import numpy as np
import ml_dtypes


def mxq(x, axis, fmt="e4m3"):
    dtype, down = {"e4m3": (ml_dtypes.float8_e4m3fn, 7), "e5m2": (ml_dtypes.float8_e5m2, 14)}[fmt]
    v = np.moveaxis(np.asarray(x, np.float32).astype(ml_dtypes.bfloat16).astype(np.float64), axis, -1)
    blocks = v.reshape(v.shape[:-1] + (-1, 32))
    amax = np.abs(blocks).max(-1, keepdims=True)
    byte = np.maximum(np.where(amax > 0, np.frexp(amax)[1] - 1 + 127, 0) - down, 1)
    scale = np.exp2(byte - 127.0)
    codes = (blocks / scale).astype(np.float32).astype(dtype).astype(np.float64)
    return np.moveaxis((codes * scale).reshape(v.shape), -1, axis)


WIDE = False


def mx_kscale(k):
    if not WIDE:
        return np.ones(k)
    levels = np.array([10, -10, 5, -5, 0])
    if k % 512:
        return np.exp2(np.random.permutation(np.resize(levels, k // 32))).repeat(32)
    a = np.empty((k // 512, 16))
    for p in range(k // 512):
        a[p, :8] = np.random.permutation(np.resize(levels, 8))
        for g in range(8):
            far = levels[np.abs(levels - a[p, g]) >= 10]
            a[p, g + 8] = far[np.random.randint(len(far))]
    return np.exp2(a.ravel()).repeat(32)


def f64(x):
    return np.asarray(x).astype(np.float64)


def striped(idx):
    return np.tile(idx.reshape(-1, 16).T, (8, 1)).astype(np.uint16)


def unstriped(offs):
    return offs[:16].T.reshape(-1).astype(np.int64)


def pack_weight(w):
    k, n = w.shape
    w = f64(np.asarray(w, np.float32).astype(ml_dtypes.bfloat16)).reshape(k // 32, 32, n)
    amax = np.abs(w).max(1)
    byte = np.clip(np.where(amax > 0, np.frexp(amax)[1] - 1 + 127 - 7, 1), 1, 254)
    scaled = (w * np.exp2(127.0 - byte)[:, None, :]).reshape(k, n).astype(np.float32)
    words = np.ascontiguousarray(scaled.reshape(k // 512, 128, 4, n).transpose(0, 1, 3, 2)).astype(ml_dtypes.float8_e4m3fn).view(np.uint8)
    return words, np.ascontiguousarray(byte.astype(np.uint8).reshape(k // 512, 16, n))


def unpack_weight(words, scales):
    g, p, n, _ = words.shape
    vals = np.ascontiguousarray(words).view(ml_dtypes.float8_e4m3fn).astype(np.float64) * np.repeat(np.exp2(scales.astype(np.float64) - 127.0), 8, axis=1)[..., None]
    return vals.transpose(0, 1, 3, 2).reshape(g * 512, n)


def relu(v):
    return np.maximum(v, 0.0)


K, T, S, N = 1024, 1024, 512, 256
P = 2 ** 7


def setup_inputs():
    n = np.random.standard_normal
    s = mx_kscale(K)[:, None]
    packed_xT = pack_weight(n((K, T)) * s)
    return {
        "x_words": packed_xT[0],
        "x_scales": packed_xT[1],
        "tscale": np.tile(np.random.uniform(0.25, 2.0, T), (P, 1)).astype(np.float32),
        "cscale": np.random.uniform(0.5, 1.5, (N, 1)).astype(np.float32),
        "w1": (n((K, N)) / np.sqrt(K) / s).astype(np.float32),
        "offs": striped(np.random.permutation(T)[:S]),
    }


def reference(x_words, x_scales, tscale, cscale, w1, offs):
    xq = unpack_weight(x_words, x_scales)[:, unstriped(offs)]
    y = mxq(f64(w1), 0, "e4m3").T @ xq
    tg = f64(tscale)[:1][:, unstriped(offs)]
    return relu((f64(cscale) * y) * tg)

@@ -1,0 +1,137 @@
+from contextlib import ExitStack
+
+import concourse.mybir as mybir
+from concourse.masks import make_identity
+
+K, T, S, N = 1024, 1024, 512, 256
+FLOPS = 2 * K * S * N
+
+F32 = mybir.dt.float32
+BF16 = mybir.dt.bfloat16
+I32 = mybir.dt.int32
+U32 = mybir.dt.uint32
+U16 = mybir.dt.uint16
+U8 = mybir.dt.uint8
+FP8X4 = mybir.dt.float8_e4m3fn_x4
+MULT = mybir.AluOpType.mult
+COPY = mybir.ActivationFunctionType.Copy
+RELU = mybir.ActivationFunctionType.Relu
+
+P = 128
+PACK = 4
+K_PASS = P * PACK
+PASSES = K // K_PASS
+BLOCKS = N // P
+HALF = S // 2
+HALVES = 2
+BANK = 512
+
+
+def tile_picked_tokscale_relu_p_kernel(tc, x_words, x_scales, tscale, cscale, w1, offs, out):
+    nc = tc.nc
+    with ExitStack() as ctx:
+        keep = ctx.enter_context(tc.tile_pool(name="keep", bufs=1))
+        psum = ctx.enter_context(tc.psum_pool(name="psum", bufs=1))
+
+        offsets = keep.tile([P, S // 16], U16, name="offsets")
+        nc.sync.dma_start(offsets[:], offs)
+
+        scale_table = keep.tile([P, T], U8, name="scale_table", align_bytes=64)
+        nc.vector.memset(scale_table[:].bitcast(I32), 0)
+        for q in range(4):
+            nc.sync.dma_start(
+                scale_table[32 * q : 32 * q + 4 * PASSES, :].bitcast(I32),
+                x_scales[:, 4 * q : 4 * q + 4, :].bitcast(I32),
+            )
+
+        t_cols = keep.tile([P, T // BANK, PACK], F32, name="t_cols")
+        nc.gpsimd.dma_start(t_cols[:], tscale[0].rearrange("(h n j) -> n h j", n=P, j=PACK))
+        c_cols = keep.tile([P, BLOCKS], F32, name="c_cols")
+        with nc.allow_non_contiguous_dma(reason="256 channel scales, one a partition"):
+            nc.gpsimd.dma_start(c_cols[:], cscale.rearrange("(b p) o -> p (b o)", p=P))
+
+        word_table = [keep.tile([P, T], U32, name="word_table%d" % z, align_bytes=64) for z in range(PASSES)]
+        w_raw = [keep.tile([P, PACK, N], F32, name="w_raw%d" % z, align_bytes=64) for z in range(PASSES)]
+
+        def load_words(z):
+            nc.sync.dma_start(word_table[z][:].bitcast(I32), x_words[z].rearrange("p n t -> p (n t)").bitcast(I32))
+
+        def load_weights(z):
+            nc.sync.dma_start(w_raw[z][:], w1[z * K_PASS : (z + 1) * K_PASS, :].rearrange("(p j) m -> p j m", j=PACK))
+
+        load_words(0)
+        load_weights(0)
+        load_weights(1)
+        load_words(1)
+
+        identity = keep.tile([P, P], F32, name="identity")
+        make_identity(nc, identity[:])
+        t_table = keep.tile([P, T], F32, name="t_table", align_bytes=64)
+        for h in range(T // BANK):
+            spread = psum.tile([P, PACK, P], F32, name="spread%d" % h)
+            for j in range(PACK):
+                nc.tensor.transpose(spread[:, j, :], t_cols[:, h, j : j + 1].to_broadcast([P, P]), identity[:])
+            nc.scalar.activation(
+                t_table[:, h * BANK : (h + 1) * BANK].rearrange("p (n j) -> p n j", j=PACK),
+                spread[:].rearrange("p j n -> p n j"),
+                COPY,
+            )
+
+        x_scale = keep.tile([P, S], U8, name="x_scale", align_bytes=64)
+        nc.vector.tensor_copy(x_scale[:], scale_table[:].indirect(offsets[:]))
+        x_first = keep.tile([P, S], U32, name="x_first", align_bytes=64)
+        nc.vector.tensor_copy(x_first[:], word_table[0][:].indirect(offsets[:]))
+        t_picked = keep.tile([P, S], F32, name="t_picked", align_bytes=64)
+        nc.vector.tensor_copy(t_picked[:], t_table[:].indirect(offsets[:]))
+
+        w_codes = {}
+        w_scale = {}
+
+        def quantize_weights(z, b):
+            grouped = keep.tile([P, P, PACK], BF16, name="grouped%d%d" % (z, b), align_bytes=64)
+            nc.scalar.copy(
+                grouped[:].rearrange("p (c i) t -> p c t i", i=4),
+                w_raw[z][:, :, b * P : (b + 1) * P].rearrange("p t (c i) -> p c t i", i=4),
+            )
+            w_codes[z, b] = keep.tile([P, P], U32, name="w_codes%d%d" % (z, b), align_bytes=64)
+            w_scale[z, b] = keep.tile([P, P], U8, name="w_scale%d%d" % (z, b), align_bytes=64)
+            nc.vector.quantize_mx(w_codes[z, b][:].bitcast(FP8X4), w_scale[z, b][:], grouped[:].rearrange("p m t -> p (m t)"))
+
+        acc = {}
+
+        def multiply(z, b, h, words):
+            nc.tensor.matmul_mx(
+                acc[b, h][:],
+                lhsT=w_codes[z, b][:].bitcast(FP8X4),
+                lhsT_scale=w_scale[z, b][:],
+                rhs=words.bitcast(FP8X4),
+                rhs_scale=x_scale[4 * z :, h * HALF : (h + 1) * HALF],
+                start=(z == 0),
+                stop=(z == PASSES - 1),
+            )
+
+        for b in range(BLOCKS):
+            quantize_weights(0, b)
+            for h in range(HALVES):
+                acc[b, h] = psum.tile([P, HALF], F32, name="acc%d%d" % (b, h))
+                multiply(0, b, h, x_first[:, h * HALF : (h + 1) * HALF])
+        for b in range(BLOCKS):
+            quantize_weights(1, b)
+
+        x_second = []
+        for h in range(HALVES):
+            picked = keep.tile([P, HALF], U32, name="x_second%d" % h, align_bytes=64)
+            nc.vector.tensor_copy(picked[:], word_table[1][:].indirect(offsets[:, h * HALF // 16 : (h + 1) * HALF // 16]))
+            x_second.append(picked)
+            for b in range(BLOCKS):
+                multiply(1, b, h, picked[:])
+
+        for h in range(HALVES):
+            for b in range(BLOCKS):
+                scaled = keep.tile([P, HALF], F32, name="scaled%d%d" % (b, h), align_bytes=64)
+                nc.vector.scalar_tensor_tensor(
+                    scaled[:], acc[b, h][:], c_cols[:, b : b + 1], t_picked[:, h * HALF : (h + 1) * HALF], MULT, MULT
+                )
+                result = keep.tile([P, HALF], F32, name="result%d%d" % (b, h), align_bytes=64)
+                nc.scalar.activation(result[:], scaled[:], RELU)
+                nc.sync.dma_start(out[b * P : (b + 1) * P, h * HALF : (h + 1) * HALF], result[:])

@@ -24,6 +24,7 @@ PASSES = K // K_PASS
 BLOCKS = N // P
 HALF = S // 2
 HALVES = 2
+QUARTER = S // 4
 BANK = 512
 
 
@@ -36,6 +37,9 @@ def tile_picked_tokscale_relu_p_kernel(tc, x_words, x_scales, tscale, cscale, w1
         offsets = keep.tile([P, S // 16], U16, name="offsets")
         nc.sync.dma_start(offsets[:], offs)
 
+        t_cols = keep.tile([P, T // P], F32, name="t_cols", tag="slot_b", align_bytes=64)
+        nc.scalar.dma_start(t_cols[:], tscale[0].rearrange("(n j) -> n j", n=P))
+
         scale_table = keep.tile([P, T], U8, name="scale_table", align_bytes=64)
         nc.vector.memset(scale_table[:].bitcast(I32), 0)
         for q in range(4):
@@ -44,14 +48,10 @@ def tile_picked_tokscale_relu_p_kernel(tc, x_words, x_scales, tscale, cscale, w1
                 x_scales[:, 4 * q : 4 * q + 4, :].bitcast(I32),
             )
 
-        t_cols = keep.tile([P, T // BANK, PACK], F32, name="t_cols")
-        nc.gpsimd.dma_start(t_cols[:], tscale[0].rearrange("(h n j) -> n h j", n=P, j=PACK))
         c_cols = keep.tile([P, BLOCKS], F32, name="c_cols")
-        with nc.allow_non_contiguous_dma(reason="256 channel scales, one a partition"):
-            nc.gpsimd.dma_start(c_cols[:], cscale.rearrange("(b p) o -> p (b o)", p=P))
 
         word_table = [keep.tile([P, T], U32, name="word_table%d" % z, align_bytes=64) for z in range(PASSES)]
-        w_raw = [keep.tile([P, PACK, N], F32, name="w_raw%d" % z, align_bytes=64) for z in range(PASSES)]
+        w_raw = [keep.tile([P, PACK, N], F32, name="w_raw%d" % z, tag="w_raw%d" % z, align_bytes=64) for z in range(PASSES)]
 
         def load_words(z):
             nc.sync.dma_start(word_table[z][:].bitcast(I32), x_words[z].rearrange("p n t -> p (n t)").bitcast(I32))
@@ -63,16 +63,18 @@ def tile_picked_tokscale_relu_p_kernel(tc, x_words, x_scales, tscale, cscale, w1
         load_weights(0)
         load_weights(1)
         load_words(1)
+        with nc.allow_non_contiguous_dma(reason="256 channel scales, one a partition"):
+            nc.sync.dma_start(c_cols[:], cscale.rearrange("(b p) o -> p (b o)", p=P))
 
-        identity = keep.tile([P, P], F32, name="identity")
+        identity = keep.tile([P, P], F32, name="identity", tag="slot_a", align_bytes=64)
         make_identity(nc, identity[:])
         t_table = keep.tile([P, T], F32, name="t_table", align_bytes=64)
         for h in range(T // BANK):
             spread = psum.tile([P, PACK, P], F32, name="spread%d" % h)
             for j in range(PACK):
-                nc.tensor.transpose(spread[:, j, :], t_cols[:, h, j : j + 1].to_broadcast([P, P]), identity[:])
+                nc.tensor.transpose(spread[:, j, :], t_cols[:, PACK * h + j : PACK * h + j + 1].to_broadcast([P, P]), identity[:])
             nc.scalar.activation(
-                t_table[:, h * BANK : (h + 1) * BANK].rearrange("p (n j) -> p n j", j=PACK),
+                t_table[:].rearrange("p (n j) -> p n j", n=P)[:, :, PACK * h : PACK * (h + 1)],
                 spread[:].rearrange("p j n -> p n j"),
                 COPY,
             )
@@ -87,51 +89,68 @@ def tile_picked_tokscale_relu_p_kernel(tc, x_words, x_scales, tscale, cscale, w1
         w_codes = {}
         w_scale = {}
 
-        def quantize_weights(z, b):
-            grouped = keep.tile([P, P, PACK], BF16, name="grouped%d%d" % (z, b), align_bytes=64)
-            nc.scalar.copy(
+        def quantize_weights(z, first, count, slot, copy):
+            width = count * P
+            grouped = keep.tile([P, width, PACK], BF16, name="grouped%d%d" % (z, first), tag=slot, align_bytes=64)
+            copy(
                 grouped[:].rearrange("p (c i) t -> p c t i", i=4),
-                w_raw[z][:, :, b * P : (b + 1) * P].rearrange("p t (c i) -> p c t i", i=4),
+                w_raw[z][:, :, first * P : first * P + width].rearrange("p t (c i) -> p c t i", i=4),
             )
-            w_codes[z, b] = keep.tile([P, P], U32, name="w_codes%d%d" % (z, b), align_bytes=64)
-            w_scale[z, b] = keep.tile([P, P], U8, name="w_scale%d%d" % (z, b), align_bytes=64)
-            nc.vector.quantize_mx(w_codes[z, b][:].bitcast(FP8X4), w_scale[z, b][:], grouped[:].rearrange("p m t -> p (m t)"))
+            codes = keep.tile([P, width], U32, name="w_codes%d%d" % (z, first), align_bytes=64)
+            scale = keep.tile([P, width], U8, name="w_scale%d%d" % (z, first), align_bytes=64)
+            nc.vector.quantize_mx(codes[:].bitcast(FP8X4), scale[:], grouped[:].rearrange("p m t -> p (m t)"))
+            for i in range(count):
+                w_codes[z, first + i] = codes[:, i * P : (i + 1) * P]
+                w_scale[z, first + i] = scale[:, i * P : (i + 1) * P]
 
         acc = {}
 
         def multiply(z, b, h, words):
             nc.tensor.matmul_mx(
                 acc[b, h][:],
-                lhsT=w_codes[z, b][:].bitcast(FP8X4),
-                lhsT_scale=w_scale[z, b][:],
+                lhsT=w_codes[z, b].bitcast(FP8X4),
+                lhsT_scale=w_scale[z, b],
                 rhs=words.bitcast(FP8X4),
                 rhs_scale=x_scale[4 * z :, h * HALF : (h + 1) * HALF],
                 start=(z == 0),
                 stop=(z == PASSES - 1),
             )
 
+        quantize_weights(0, 0, BLOCKS, "slot_a", nc.scalar.copy)
         for b in range(BLOCKS):
-            quantize_weights(0, b)
             for h in range(HALVES):
                 acc[b, h] = psum.tile([P, HALF], F32, name="acc%d%d" % (b, h))
                 multiply(0, b, h, x_first[:, h * HALF : (h + 1) * HALF])
-        for b in range(BLOCKS):
-            quantize_weights(1, b)
+        quantize_weights(1, 0, 1, "slot_b", nc.scalar.copy)
+        quantize_weights(1, 1, 1, "w_raw0", nc.vector.tensor_copy)
 
-        x_second = []
+        x_second = keep.tile([P, S], U32, name="x_second", tag="slot_b", align_bytes=64)
         for h in range(HALVES):
-            picked = keep.tile([P, HALF], U32, name="x_second%d" % h, align_bytes=64)
-            nc.vector.tensor_copy(picked[:], word_table[1][:].indirect(offsets[:, h * HALF // 16 : (h + 1) * HALF // 16]))
-            x_second.append(picked)
-            for b in range(BLOCKS):
-                multiply(1, b, h, picked[:])
-
+            nc.vector.tensor_copy(
+                x_second[:, h * HALF : (h + 1) * HALF],
+                word_table[1][:].indirect(offsets[:, h * HALF // 16 : (h + 1) * HALF // 16]),
+            )
         for h in range(HALVES):
             for b in range(BLOCKS):
-                scaled = keep.tile([P, HALF], F32, name="scaled%d%d" % (b, h), align_bytes=64)
-                nc.vector.scalar_tensor_tensor(
-                    scaled[:], acc[b, h][:], c_cols[:, b : b + 1], t_picked[:, h * HALF : (h + 1) * HALF], MULT, MULT
-                )
-                result = keep.tile([P, HALF], F32, name="result%d%d" % (b, h), align_bytes=64)
-                nc.scalar.activation(result[:], scaled[:], RELU)
-                nc.sync.dma_start(out[b * P : (b + 1) * P, h * HALF : (h + 1) * HALF], result[:])
+                multiply(1, b, h, x_second[:, h * HALF : (h + 1) * HALF])
+
+        def scale(b, column, width):
+            h, start = divmod(column, HALF)
+            scaled = keep.tile([P, width], F32, name="scaled%d_%d" % (b, column), align_bytes=64)
+            nc.vector.scalar_tensor_tensor(
+                scaled[:], acc[b, h][:, start : start + width], c_cols[:, b : b + 1], t_picked[:, column : column + width], MULT, MULT
+            )
+            return scaled
+
+        for b, h in ((0, 0), (1, 0), (0, 1)):
+            scaled = scale(b, h * HALF, HALF)
+            result = keep.tile([P, HALF], F32, name="result%d%d" % (b, h), align_bytes=64)
+            nc.scalar.activation(result[:], scaled[:], RELU)
+            nc.sync.dma_start(out[b * P : (b + 1) * P, h * HALF : (h + 1) * HALF], result[:])
+
+        columns = (HALF, HALF + QUARTER)
+        last = [scale(1, column, QUARTER) for column in columns]
+        for column, scaled, queue in zip(columns, last, (nc.sync, nc.scalar)):
+            result = keep.tile([P, QUARTER], F32, name="result_last%d" % column, align_bytes=64)
+            nc.vector.tensor_scalar_max(result[:], scaled[:], 0.0)
+            queue.dma_start(out[P:N, column : column + QUARTER], result[:])

@@ -24,7 +24,6 @@ PASSES = K // K_PASS
 BLOCKS = N // P
 HALF = S // 2
 HALVES = 2
-QUARTER = S // 4
 BANK = 512
 
 
@@ -38,7 +37,7 @@ def tile_picked_tokscale_relu_p_kernel(tc, x_words, x_scales, tscale, cscale, w1
         nc.sync.dma_start(offsets[:], offs)
 
         t_cols = keep.tile([P, T // P], F32, name="t_cols", tag="slot_b", align_bytes=64)
-        nc.scalar.dma_start(t_cols[:], tscale[0].rearrange("(n j) -> n j", n=P))
+        nc.sync.dma_start(t_cols[:], tscale[0].rearrange("(n j) -> n j", n=P))
 
         scale_table = keep.tile([P, T], U8, name="scale_table", align_bytes=64)
         nc.vector.memset(scale_table[:].bitcast(I32), 0)
@@ -134,23 +133,17 @@ def tile_picked_tokscale_relu_p_kernel(tc, x_words, x_scales, tscale, cscale, w1
             for b in range(BLOCKS):
                 multiply(1, b, h, x_second[:, h * HALF : (h + 1) * HALF])
 
-        def scale(b, column, width):
-            h, start = divmod(column, HALF)
+        def finish(b, h, start, width):
+            column = h * HALF + start
             scaled = keep.tile([P, width], F32, name="scaled%d_%d" % (b, column), align_bytes=64)
             nc.vector.scalar_tensor_tensor(
                 scaled[:], acc[b, h][:, start : start + width], c_cols[:, b : b + 1], t_picked[:, column : column + width], MULT, MULT
             )
-            return scaled
-
-        for b, h in ((0, 0), (1, 0), (0, 1)):
-            scaled = scale(b, h * HALF, HALF)
-            result = keep.tile([P, HALF], F32, name="result%d%d" % (b, h), align_bytes=64)
+            result = keep.tile([P, width], F32, name="result%d_%d" % (b, column), align_bytes=64)
             nc.scalar.activation(result[:], scaled[:], RELU)
-            nc.sync.dma_start(out[b * P : (b + 1) * P, h * HALF : (h + 1) * HALF], result[:])
+            nc.sync.dma_start(out[b * P : (b + 1) * P, column : column + width], result[:])
 
-        columns = (HALF, HALF + QUARTER)
-        last = [scale(1, column, QUARTER) for column in columns]
-        for column, scaled, queue in zip(columns, last, (nc.sync, nc.scalar)):
-            result = keep.tile([P, QUARTER], F32, name="result_last%d" % column, align_bytes=64)
-            nc.vector.tensor_scalar_max(result[:], scaled[:], 0.0)
-            queue.dma_start(out[P:N, column : column + QUARTER], result[:])
+        finish(0, 0, 0, HALF)
+        finish(1, 0, 0, HALF)
+        finish(0, 1, 0, HALF)
+        finish(1, 1, 0, HALF)

@@ -36,16 +36,12 @@ def tile_picked_tokscale_relu_p_kernel(tc, x_words, x_scales, tscale, cscale, w1
         offsets = keep.tile([P, S // 16], U16, name="offsets")
         nc.sync.dma_start(offsets[:], offs)
 
-        t_cols = keep.tile([P, T // P], F32, name="t_cols", tag="slot_b", align_bytes=64)
-        nc.sync.dma_start(t_cols[:], tscale[0].rearrange("(n j) -> n j", n=P))
+        t_table = keep.tile([P, T], F32, name="t_table", align_bytes=64)
+        nc.sync.dma_start(t_table[P - 1 : P, :], tscale[0:1, :])
 
         scale_table = keep.tile([P, T], U8, name="scale_table", align_bytes=64)
-        nc.vector.memset(scale_table[:].bitcast(I32), 0)
-        for q in range(4):
-            nc.sync.dma_start(
-                scale_table[32 * q : 32 * q + 4 * PASSES, :].bitcast(I32),
-                x_scales[:, 4 * q : 4 * q + 4, :].bitcast(I32),
-            )
+        nc.gpsimd.memset(scale_table[:].bitcast(I32), 0)
+        nc.vector.memset(t_table[0 : P - 1, :], 0.0)
 
         c_cols = keep.tile([P, BLOCKS], F32, name="c_cols")
 
@@ -59,39 +55,34 @@ def tile_picked_tokscale_relu_p_kernel(tc, x_words, x_scales, tscale, cscale, w1
             nc.sync.dma_start(w_raw[z][:], w1[z * K_PASS : (z + 1) * K_PASS, :].rearrange("(p j) m -> p j m", j=PACK))
 
         load_words(0)
+        for q in range(4):
+            nc.sync.dma_start(
+                scale_table[32 * q : 32 * q + 4 * PASSES, :].bitcast(I32),
+                x_scales[:, 4 * q : 4 * q + 4, :].bitcast(I32),
+            )
         load_weights(0)
-        load_weights(1)
         load_words(1)
+        load_weights(1)
         with nc.allow_non_contiguous_dma(reason="256 channel scales, one a partition"):
             nc.sync.dma_start(c_cols[:], cscale.rearrange("(b p) o -> p (b o)", p=P))
 
-        identity = keep.tile([P, P], F32, name="identity", tag="slot_a", align_bytes=64)
+        identity = keep.tile([P, P], F32, name="identity", align_bytes=64)
         make_identity(nc, identity[:])
-        t_table = keep.tile([P, T], F32, name="t_table", align_bytes=64)
-        for h in range(T // BANK):
-            spread = psum.tile([P, PACK, P], F32, name="spread%d" % h)
-            for j in range(PACK):
-                nc.tensor.transpose(spread[:, j, :], t_cols[:, PACK * h + j : PACK * h + j + 1].to_broadcast([P, P]), identity[:])
-            nc.scalar.activation(
-                t_table[:].rearrange("p (n j) -> p n j", n=P)[:, :, PACK * h : PACK * (h + 1)],
-                spread[:].rearrange("p j n -> p n j"),
-                COPY,
-            )
 
-        x_scale = keep.tile([P, S], U8, name="x_scale", align_bytes=64)
-        nc.vector.tensor_copy(x_scale[:], scale_table[:].indirect(offsets[:]))
+        t_row = keep.tile([P, S], F32, name="t_row", tag="slot_a", align_bytes=64)
+        nc.vector.tensor_copy(t_row[:], t_table[:].indirect(offsets[:]))
         x_first = keep.tile([P, S], U32, name="x_first", align_bytes=64)
         nc.vector.tensor_copy(x_first[:], word_table[0][:].indirect(offsets[:]))
-        t_picked = keep.tile([P, S], F32, name="t_picked", align_bytes=64)
-        nc.vector.tensor_copy(t_picked[:], t_table[:].indirect(offsets[:]))
+        x_scale = keep.tile([P, S], U8, name="x_scale", align_bytes=64)
+        nc.vector.tensor_copy(x_scale[:], scale_table[:].indirect(offsets[:]))
 
         w_codes = {}
         w_scale = {}
 
-        def quantize_weights(z, first, count, slot, copy):
+        def quantize_weights(z, first, count, slot):
             width = count * P
             grouped = keep.tile([P, width, PACK], BF16, name="grouped%d%d" % (z, first), tag=slot, align_bytes=64)
-            copy(
+            nc.scalar.copy(
                 grouped[:].rearrange("p (c i) t -> p c t i", i=4),
                 w_raw[z][:, :, first * P : first * P + width].rearrange("p t (c i) -> p c t i", i=4),
             )
@@ -115,22 +106,28 @@ def tile_picked_tokscale_relu_p_kernel(tc, x_words, x_scales, tscale, cscale, w1
                 stop=(z == PASSES - 1),
             )
 
-        quantize_weights(0, 0, BLOCKS, "slot_a", nc.scalar.copy)
+        turned = psum.tile([P, S // P, P], F32, name="turned")
+        for j in range(S // P):
+            nc.tensor.transpose(turned[:, j, :], t_row[:, j * P : (j + 1) * P], identity[:])
+        t_cols = keep.tile([P, S // P], F32, name="t_cols", align_bytes=64)
+        nc.scalar.activation(t_cols[:], turned[:, :, P - 1], COPY)
+        spread = psum.tile([P, S // P, P], F32, name="spread")
+        for j in range(S // P):
+            nc.tensor.transpose(spread[:, j, :], t_cols[:, j : j + 1].to_broadcast([P, P]), identity[:])
+
+        quantize_weights(0, 0, BLOCKS, "slot_a")
+        t_picked = keep.tile([P, S], F32, name="t_picked", align_bytes=64)
+        nc.scalar.activation(t_picked[:], spread[:].rearrange("p j n -> p (j n)"), COPY)
         for b in range(BLOCKS):
             for h in range(HALVES):
                 acc[b, h] = psum.tile([P, HALF], F32, name="acc%d%d" % (b, h))
                 multiply(0, b, h, x_first[:, h * HALF : (h + 1) * HALF])
-        quantize_weights(1, 0, 1, "slot_b", nc.scalar.copy)
-        quantize_weights(1, 1, 1, "w_raw0", nc.vector.tensor_copy)
 
-        x_second = keep.tile([P, S], U32, name="x_second", tag="slot_b", align_bytes=64)
-        for h in range(HALVES):
-            nc.vector.tensor_copy(
-                x_second[:, h * HALF : (h + 1) * HALF],
-                word_table[1][:].indirect(offsets[:, h * HALF // 16 : (h + 1) * HALF // 16]),
-            )
-        for h in range(HALVES):
-            for b in range(BLOCKS):
+        x_second = keep.tile([P, S], U32, name="x_second", tag="w_raw0", align_bytes=64)
+        nc.vector.tensor_copy(x_second[:], word_table[1][:].indirect(offsets[:]))
+        for b in range(BLOCKS):
+            quantize_weights(1, b, 1, "grouped1%d" % b)
+            for h in range(HALVES):
                 multiply(1, b, h, x_second[:, h * HALF : (h + 1) * HALF])
 
         def finish(b, h, start, width):
@@ -144,6 +141,6 @@ def tile_picked_tokscale_relu_p_kernel(tc, x_words, x_scales, tscale, cscale, w1
             nc.sync.dma_start(out[b * P : (b + 1) * P, column : column + width], result[:])
 
         finish(0, 0, 0, HALF)
-        finish(1, 0, 0, HALF)
         finish(0, 1, 0, HALF)
+        finish(1, 0, 0, HALF)
         finish(1, 1, 0, HALF)

@@ -54,12 +54,12 @@ def tile_picked_tokscale_relu_p_kernel(tc, x_words, x_scales, tscale, cscale, w1
         def load_weights(z):
             nc.sync.dma_start(w_raw[z][:], w1[z * K_PASS : (z + 1) * K_PASS, :].rearrange("(p j) m -> p j m", j=PACK))
 
-        load_words(0)
         for q in range(4):
             nc.sync.dma_start(
                 scale_table[32 * q : 32 * q + 4 * PASSES, :].bitcast(I32),
                 x_scales[:, 4 * q : 4 * q + 4, :].bitcast(I32),
             )
+        load_words(0)
         load_weights(0)
         load_words(1)
         load_weights(1)
@@ -71,21 +71,24 @@ def tile_picked_tokscale_relu_p_kernel(tc, x_words, x_scales, tscale, cscale, w1
 
         t_row = keep.tile([P, S], F32, name="t_row", tag="slot_a", align_bytes=64)
         nc.vector.tensor_copy(t_row[:], t_table[:].indirect(offsets[:]))
-        x_first = keep.tile([P, S], U32, name="x_first", align_bytes=64)
-        nc.vector.tensor_copy(x_first[:], word_table[0][:].indirect(offsets[:]))
         x_scale = keep.tile([P, S], U8, name="x_scale", align_bytes=64)
         nc.vector.tensor_copy(x_scale[:], scale_table[:].indirect(offsets[:]))
+        x_first = keep.tile([P, S], U32, name="x_first", align_bytes=64)
+        nc.vector.tensor_copy(x_first[:], word_table[0][:].indirect(offsets[:]))
 
         w_codes = {}
         w_scale = {}
 
-        def quantize_weights(z, first, count, slot):
+        def quantize_weights(z, first, count, slot, on_vector=0):
             width = count * P
             grouped = keep.tile([P, width, PACK], BF16, name="grouped%d%d" % (z, first), tag=slot, align_bytes=64)
-            nc.scalar.copy(
-                grouped[:].rearrange("p (c i) t -> p c t i", i=4),
-                w_raw[z][:, :, first * P : first * P + width].rearrange("p t (c i) -> p c t i", i=4),
-            )
+            split = width - on_vector
+            for copy, start, stop in ((nc.scalar.copy, 0, split), (nc.vector.tensor_copy, split, width)):
+                if stop > start:
+                    copy(
+                        grouped[:, start:stop, :].rearrange("p (c i) t -> p c t i", i=4),
+                        w_raw[z][:, :, first * P + start : first * P + stop].rearrange("p t (c i) -> p c t i", i=4),
+                    )
             codes = keep.tile([P, width], U32, name="w_codes%d%d" % (z, first), align_bytes=64)
             scale = keep.tile([P, width], U8, name="w_scale%d%d" % (z, first), align_bytes=64)
             nc.vector.quantize_mx(codes[:].bitcast(FP8X4), scale[:], grouped[:].rearrange("p m t -> p (m t)"))
@@ -126,7 +129,7 @@ def tile_picked_tokscale_relu_p_kernel(tc, x_words, x_scales, tscale, cscale, w1
         x_second = keep.tile([P, S], U32, name="x_second", tag="w_raw0", align_bytes=64)
         nc.vector.tensor_copy(x_second[:], word_table[1][:].indirect(offsets[:]))
         for b in range(BLOCKS):
-            quantize_weights(1, b, 1, "grouped1%d" % b)
+            quantize_weights(1, b, 1, ("slot_b", "slot_a")[b], on_vector=b * P // 2)
             for h in range(HALVES):
                 multiply(1, b, h, x_second[:, h * HALF : (h + 1) * HALF])
 

@@ -54,15 +54,15 @@ def tile_picked_tokscale_relu_p_kernel(tc, x_words, x_scales, tscale, cscale, w1
         def load_weights(z):
             nc.sync.dma_start(w_raw[z][:], w1[z * K_PASS : (z + 1) * K_PASS, :].rearrange("(p j) m -> p j m", j=PACK))
 
+        load_words(0)
         for q in range(4):
             nc.sync.dma_start(
                 scale_table[32 * q : 32 * q + 4 * PASSES, :].bitcast(I32),
                 x_scales[:, 4 * q : 4 * q + 4, :].bitcast(I32),
             )
-        load_words(0)
         load_weights(0)
-        load_words(1)
         load_weights(1)
+        load_words(1)
         with nc.allow_non_contiguous_dma(reason="256 channel scales, one a partition"):
             nc.sync.dma_start(c_cols[:], cscale.rearrange("(b p) o -> p (b o)", p=P))
 
@@ -71,30 +71,32 @@ def tile_picked_tokscale_relu_p_kernel(tc, x_words, x_scales, tscale, cscale, w1
 
         t_row = keep.tile([P, S], F32, name="t_row", tag="slot_a", align_bytes=64)
         nc.vector.tensor_copy(t_row[:], t_table[:].indirect(offsets[:]))
-        x_scale = keep.tile([P, S], U8, name="x_scale", align_bytes=64)
-        nc.vector.tensor_copy(x_scale[:], scale_table[:].indirect(offsets[:]))
         x_first = keep.tile([P, S], U32, name="x_first", align_bytes=64)
         nc.vector.tensor_copy(x_first[:], word_table[0][:].indirect(offsets[:]))
+        x_scale = keep.tile([P, S], U8, name="x_scale", align_bytes=64)
+        nc.vector.tensor_copy(x_scale[:], scale_table[:].indirect(offsets[:]))
 
         w_codes = {}
         w_scale = {}
 
-        def quantize_weights(z, first, count, slot, on_vector=0):
-            width = count * P
-            grouped = keep.tile([P, width, PACK], BF16, name="grouped%d%d" % (z, first), tag=slot, align_bytes=64)
+        def lay_out(z, first, width, slot, on_vector):
+            grouped = keep.tile([P, width, PACK], BF16, name="grouped%d_%d" % (z, first), tag=slot, align_bytes=64)
             split = width - on_vector
             for copy, start, stop in ((nc.scalar.copy, 0, split), (nc.vector.tensor_copy, split, width)):
                 if stop > start:
                     copy(
                         grouped[:, start:stop, :].rearrange("p (c i) t -> p c t i", i=4),
-                        w_raw[z][:, :, first * P + start : first * P + stop].rearrange("p t (c i) -> p c t i", i=4),
+                        w_raw[z][:, :, first + start : first + stop].rearrange("p t (c i) -> p c t i", i=4),
                     )
-            codes = keep.tile([P, width], U32, name="w_codes%d%d" % (z, first), align_bytes=64)
-            scale = keep.tile([P, width], U8, name="w_scale%d%d" % (z, first), align_bytes=64)
+            return grouped
+
+        def quantize(z, first, width, grouped):
+            codes = keep.tile([P, width], U32, name="w_codes%d_%d" % (z, first), align_bytes=64)
+            scale = keep.tile([P, width], U8, name="w_scale%d_%d" % (z, first), align_bytes=64)
             nc.vector.quantize_mx(codes[:].bitcast(FP8X4), scale[:], grouped[:].rearrange("p m t -> p (m t)"))
-            for i in range(count):
-                w_codes[z, first + i] = codes[:, i * P : (i + 1) * P]
-                w_scale[z, first + i] = scale[:, i * P : (i + 1) * P]
+            for start in range(0, width, P):
+                w_codes[z, (first + start) // P] = codes[:, start : start + P]
+                w_scale[z, (first + start) // P] = scale[:, start : start + P]
 
         acc = {}
 
@@ -118,19 +120,30 @@ def tile_picked_tokscale_relu_p_kernel(tc, x_words, x_scales, tscale, cscale, w1
         for j in range(S // P):
             nc.tensor.transpose(spread[:, j, :], t_cols[:, j : j + 1].to_broadcast([P, P]), identity[:])
 
-        quantize_weights(0, 0, BLOCKS, "slot_a")
-        t_picked = keep.tile([P, S], F32, name="t_picked", align_bytes=64)
-        nc.scalar.activation(t_picked[:], spread[:].rearrange("p j n -> p (j n)"), COPY)
         for b in range(BLOCKS):
             for h in range(HALVES):
                 acc[b, h] = psum.tile([P, HALF], F32, name="acc%d%d" % (b, h))
+
+        quantize(0, 0, N, lay_out(0, 0, N, "slot_a", 0))
+        for h in range(HALVES):
+            for b in range(BLOCKS):
                 multiply(0, b, h, x_first[:, h * HALF : (h + 1) * HALF])
 
-        x_second = keep.tile([P, S], U32, name="x_second", tag="w_raw0", align_bytes=64)
-        nc.vector.tensor_copy(x_second[:], word_table[1][:].indirect(offsets[:]))
-        for b in range(BLOCKS):
-            quantize_weights(1, b, 1, ("slot_b", "slot_a")[b], on_vector=b * P // 2)
-            for h in range(HALVES):
+        grouped_low = lay_out(1, 0, P, "slot_b", 0)
+        grouped_high = lay_out(1, P, P, "slot_a", P // 2)
+        quantize(1, 0, P, grouped_low)
+        quantize(1, P, P, grouped_high)
+
+        t_picked = keep.tile([P, S], F32, name="t_picked", tag="w_raw1", align_bytes=64)
+        nc.scalar.activation(t_picked[:], spread[:].rearrange("p j n -> p (j n)"), COPY)
+
+        x_second = keep.tile([P, S], U32, name="x_second", tag="slot_b", align_bytes=64)
+        for h in range(HALVES):
+            nc.vector.tensor_copy(
+                x_second[:, h * HALF : (h + 1) * HALF],
+                word_table[1][:].indirect(offsets[:, h * HALF // 16 : (h + 1) * HALF // 16]),
+            )
+            for b in range(BLOCKS):
                 multiply(1, b, h, x_second[:, h * HALF : (h + 1) * HALF])
 
         def finish(b, h, start, width):
@@ -144,6 +157,6 @@ def tile_picked_tokscale_relu_p_kernel(tc, x_words, x_scales, tscale, cscale, w1
             nc.sync.dma_start(out[b * P : (b + 1) * P, column : column + width], result[:])
 
         finish(0, 0, 0, HALF)
-        finish(0, 1, 0, HALF)
         finish(1, 0, 0, HALF)
+        finish(0, 1, 0, HALF)
         finish(1, 1, 0, HALF)

@@ -82,7 +82,7 @@ def tile_picked_tokscale_relu_p_kernel(tc, x_words, x_scales, tscale, cscale, w1
         def lay_out(z, first, width, slot, on_vector):
             grouped = keep.tile([P, width, PACK], BF16, name="grouped%d_%d" % (z, first), tag=slot, align_bytes=64)
             split = width - on_vector
-            for copy, start, stop in ((nc.scalar.copy, 0, split), (nc.vector.tensor_copy, split, width)):
+            for copy, start, stop in ((nc.scalar.copy, 0, min(P, split)), (nc.scalar.copy, P, split), (nc.vector.tensor_copy, split, width)):
                 if stop > start:
                     copy(
                         grouped[:, start:stop, :].rearrange("p (c i) t -> p c t i", i=4),
@@ -93,7 +93,7 @@ def tile_picked_tokscale_relu_p_kernel(tc, x_words, x_scales, tscale, cscale, w1
         def quantize(z, first, width, grouped):
             codes = keep.tile([P, width], U32, name="w_codes%d_%d" % (z, first), align_bytes=64)
             scale = keep.tile([P, width], U8, name="w_scale%d_%d" % (z, first), align_bytes=64)
-            nc.vector.quantize_mx(codes[:].bitcast(FP8X4), scale[:], grouped[:].rearrange("p m t -> p (m t)"))
+            nc.vector.quantize_mx(codes[:].bitcast(FP8X4), scale[:], grouped.rearrange("p m t -> p (m t)"))
             for start in range(0, width, P):
                 w_codes[z, (first + start) // P] = codes[:, start : start + P]
                 w_scale[z, (first + start) // P] = scale[:, start : start + P]
@@ -124,15 +124,17 @@ def tile_picked_tokscale_relu_p_kernel(tc, x_words, x_scales, tscale, cscale, w1
             for h in range(HALVES):
                 acc[b, h] = psum.tile([P, HALF], F32, name="acc%d%d" % (b, h))
 
-        quantize(0, 0, N, lay_out(0, 0, N, "slot_a", 0))
+        grouped_first = lay_out(0, 0, N, "slot_a", 64)
+        for b in range(BLOCKS):
+            quantize(0, b * P, P, grouped_first[:, b * P : (b + 1) * P, :])
         for h in range(HALVES):
             for b in range(BLOCKS):
                 multiply(0, b, h, x_first[:, h * HALF : (h + 1) * HALF])
 
         grouped_low = lay_out(1, 0, P, "slot_b", 0)
-        grouped_high = lay_out(1, P, P, "slot_a", P // 2)
-        quantize(1, 0, P, grouped_low)
-        quantize(1, P, P, grouped_high)
+        grouped_high = lay_out(1, P, P, "slot_a", 96)
+        quantize(1, 0, P, grouped_low[:])
+        quantize(1, P, P, grouped_high[:])
 
         t_picked = keep.tile([P, S], F32, name="t_picked", tag="w_raw1", align_bytes=64)
         nc.scalar.activation(t_picked[:], spread[:].rearrange("p j n -> p (j n)"), COPY)
@@ -159,4 +161,5 @@ def tile_picked_tokscale_relu_p_kernel(tc, x_words, x_scales, tscale, cscale, w1
         finish(0, 0, 0, HALF)
         finish(1, 0, 0, HALF)
         finish(0, 1, 0, HALF)
-        finish(1, 1, 0, HALF)
+        finish(1, 1, 0, HALF // 2)
+        finish(1, 1, HALF // 2, HALF // 2)

@@ -19,12 +19,14 @@ RELU = mybir.ActivationFunctionType.Relu
 
 P = 128
 PACK = 4
+QUADRANT = 32
+ENTRIES = 16
 K_PASS = P * PACK
 PASSES = K // K_PASS
 BLOCKS = N // P
-HALF = S // 2
 HALVES = 2
-BANK = 512
+HALF = S // HALVES
+VECTOR_SHARE = (64, 96)
 
 
 def tile_picked_tokscale_relu_p_kernel(tc, x_words, x_scales, tscale, cscale, w1, offs, out):
@@ -33,7 +35,7 @@ def tile_picked_tokscale_relu_p_kernel(tc, x_words, x_scales, tscale, cscale, w1
         keep = ctx.enter_context(tc.tile_pool(name="keep", bufs=1))
         psum = ctx.enter_context(tc.psum_pool(name="psum", bufs=1))
 
-        offsets = keep.tile([P, S // 16], U16, name="offsets")
+        offsets = keep.tile([P, S // ENTRIES], U16, name="offsets")
         nc.sync.dma_start(offsets[:], offs)
 
         t_table = keep.tile([P, T], F32, name="t_table", align_bytes=64)
@@ -55,10 +57,10 @@ def tile_picked_tokscale_relu_p_kernel(tc, x_words, x_scales, tscale, cscale, w1
             nc.sync.dma_start(w_raw[z][:], w1[z * K_PASS : (z + 1) * K_PASS, :].rearrange("(p j) m -> p j m", j=PACK))
 
         load_words(0)
-        for q in range(4):
+        for q in range(P // QUADRANT):
             nc.sync.dma_start(
-                scale_table[32 * q : 32 * q + 4 * PASSES, :].bitcast(I32),
-                x_scales[:, 4 * q : 4 * q + 4, :].bitcast(I32),
+                scale_table[QUADRANT * q : QUADRANT * q + PACK * PASSES, :].bitcast(I32),
+                x_scales[:, PACK * q : PACK * (q + 1), :].bitcast(I32),
             )
         load_weights(0)
         load_weights(1)
@@ -78,35 +80,27 @@ def tile_picked_tokscale_relu_p_kernel(tc, x_words, x_scales, tscale, cscale, w1
 
         w_codes = {}
         w_scale = {}
-
-        def lay_out(z, first, width, slot, on_vector):
-            grouped = keep.tile([P, width, PACK], BF16, name="grouped%d_%d" % (z, first), tag=slot, align_bytes=64)
-            split = width - on_vector
-            for copy, start, stop in ((nc.scalar.copy, 0, min(P, split)), (nc.scalar.copy, P, split), (nc.vector.tensor_copy, split, width)):
-                if stop > start:
-                    copy(
-                        grouped[:, start:stop, :].rearrange("p (c i) t -> p c t i", i=4),
-                        w_raw[z][:, :, first + start : first + stop].rearrange("p t (c i) -> p c t i", i=4),
-                    )
-            return grouped
-
-        def quantize(z, first, width, grouped):
-            codes = keep.tile([P, width], U32, name="w_codes%d_%d" % (z, first), align_bytes=64)
-            scale = keep.tile([P, width], U8, name="w_scale%d_%d" % (z, first), align_bytes=64)
-            nc.vector.quantize_mx(codes[:].bitcast(FP8X4), scale[:], grouped.rearrange("p m t -> p (m t)"))
-            for start in range(0, width, P):
-                w_codes[z, (first + start) // P] = codes[:, start : start + P]
-                w_scale[z, (first + start) // P] = scale[:, start : start + P]
-
         acc = {}
+
+        def lay_out(copy, grouped, z, channel):
+            width = grouped.shape[1]
+            copy(
+                grouped.rearrange("p (c i) t -> p c t i", i=PACK),
+                w_raw[z][:, :, channel : channel + width].rearrange("p t (c i) -> p c t i", i=PACK),
+            )
+
+        def quantize(z, b, grouped):
+            w_codes[z, b] = keep.tile([P, P], U32, name="w_codes%d_%d" % (z, b * P), align_bytes=64)
+            w_scale[z, b] = keep.tile([P, P], U8, name="w_scale%d_%d" % (z, b * P), align_bytes=64)
+            nc.vector.quantize_mx(w_codes[z, b][:].bitcast(FP8X4), w_scale[z, b][:], grouped.rearrange("p m t -> p (m t)"))
 
         def multiply(z, b, h, words):
             nc.tensor.matmul_mx(
                 acc[b, h][:],
-                lhsT=w_codes[z, b].bitcast(FP8X4),
-                lhsT_scale=w_scale[z, b],
-                rhs=words.bitcast(FP8X4),
-                rhs_scale=x_scale[4 * z :, h * HALF : (h + 1) * HALF],
+                lhsT=w_codes[z, b][:].bitcast(FP8X4),
+                lhsT_scale=w_scale[z, b][:],
+                rhs=words[:, h * HALF : (h + 1) * HALF].bitcast(FP8X4),
+                rhs_scale=x_scale[PACK * z :, h * HALF : (h + 1) * HALF],
                 start=(z == 0),
                 stop=(z == PASSES - 1),
             )
@@ -124,29 +118,39 @@ def tile_picked_tokscale_relu_p_kernel(tc, x_words, x_scales, tscale, cscale, w1
             for h in range(HALVES):
                 acc[b, h] = psum.tile([P, HALF], F32, name="acc%d%d" % (b, h))
 
-        grouped_first = lay_out(0, 0, N, "slot_a", 64)
-        for b in range(BLOCKS):
-            quantize(0, b * P, P, grouped_first[:, b * P : (b + 1) * P, :])
+        grouped_first = keep.tile([P, N, PACK], BF16, name="grouped0_0", tag="slot_a", align_bytes=64)
+        split = N - VECTOR_SHARE[0]
+        lay_out(nc.scalar.copy, grouped_first[:, 0:P, :], 0, 0)
+        lay_out(nc.scalar.copy, grouped_first[:, P:split, :], 0, P)
+        lay_out(nc.vector.tensor_copy, grouped_first[:, split:N, :], 0, split)
+        quantize(0, 0, grouped_first[:, 0:P, :])
+
+        grouped_low = keep.tile([P, P, PACK], BF16, name="grouped1_0", tag="slot_b", align_bytes=64)
+        lay_out(nc.scalar.copy, grouped_low[:], 1, 0)
+        grouped_high = keep.tile([P, P, PACK], BF16, name="grouped1_128", tag="w_raw0", align_bytes=64)
+        split = P - VECTOR_SHARE[1]
+        lay_out(nc.scalar.copy, grouped_high[:, 0:split, :], 1, P)
+        lay_out(nc.vector.tensor_copy, grouped_high[:, split:P, :], 1, P + split)
+        quantize(0, 1, grouped_first[:, P:N, :])
+
         for h in range(HALVES):
             for b in range(BLOCKS):
-                multiply(0, b, h, x_first[:, h * HALF : (h + 1) * HALF])
+                multiply(0, b, h, x_first)
 
-        grouped_low = lay_out(1, 0, P, "slot_b", 0)
-        grouped_high = lay_out(1, P, P, "slot_a", 96)
-        quantize(1, 0, P, grouped_low[:])
-        quantize(1, P, P, grouped_high[:])
+        quantize(1, 0, grouped_low[:])
+        quantize(1, 1, grouped_high[:])
 
-        t_picked = keep.tile([P, S], F32, name="t_picked", tag="w_raw1", align_bytes=64)
+        t_picked = keep.tile([P, S], F32, name="t_picked", tag="slot_b", align_bytes=64)
         nc.scalar.activation(t_picked[:], spread[:].rearrange("p j n -> p (j n)"), COPY)
 
-        x_second = keep.tile([P, S], U32, name="x_second", tag="slot_b", align_bytes=64)
+        x_second = keep.tile([P, S], U32, name="x_second", tag="w_raw1", align_bytes=64)
         for h in range(HALVES):
             nc.vector.tensor_copy(
                 x_second[:, h * HALF : (h + 1) * HALF],
-                word_table[1][:].indirect(offsets[:, h * HALF // 16 : (h + 1) * HALF // 16]),
+                word_table[1][:].indirect(offsets[:, h * HALF // ENTRIES : (h + 1) * HALF // ENTRIES]),
             )
             for b in range(BLOCKS):
-                multiply(1, b, h, x_second[:, h * HALF : (h + 1) * HALF])
+                multiply(1, b, h, x_second)
 
         def finish(b, h, start, width):
             column = h * HALF + start

@@ -14,6 +14,7 @@ U16 = mybir.dt.uint16
 U8 = mybir.dt.uint8
 FP8X4 = mybir.dt.float8_e4m3fn_x4
 MULT = mybir.AluOpType.mult
+MAX = mybir.AluOpType.max
 COPY = mybir.ActivationFunctionType.Copy
 RELU = mybir.ActivationFunctionType.Relu
 
@@ -24,15 +25,20 @@ ENTRIES = 16
 K_PASS = P * PACK
 PASSES = K // K_PASS
 BLOCKS = N // P
-HALVES = 2
-HALF = S // HALVES
+QUARTERS = S // P
+HALF = S // 2
+PIECES = [(0, 0, P), (0, P, P), (1, 0, HALF), (0, HALF, P), (0, HALF + P, P), (1, HALF, HALF)]
 VECTOR_SHARE = (64, 96)
+AT_SCALES = 0
+AT_RAW = (1024, 6144)
+AT_ROW = 11264
 
 
 def tile_picked_tokscale_relu_p_kernel(tc, x_words, x_scales, tscale, cscale, w1, offs, out):
     nc = tc.nc
     with ExitStack() as ctx:
         keep = ctx.enter_context(tc.tile_pool(name="keep", bufs=1))
+        shared = ctx.enter_context(tc.tile_pool(name="shared", bufs=1))
         psum = ctx.enter_context(tc.psum_pool(name="psum", bufs=1))
 
         offsets = keep.tile([P, S // ENTRIES], U16, name="offsets")
@@ -41,14 +47,14 @@ def tile_picked_tokscale_relu_p_kernel(tc, x_words, x_scales, tscale, cscale, w1
         t_table = keep.tile([P, T], F32, name="t_table", align_bytes=64)
         nc.sync.dma_start(t_table[P - 1 : P, :], tscale[0:1, :])
 
-        scale_table = keep.tile([P, T], U8, name="scale_table", align_bytes=64)
+        scale_table = shared.tile([P, T], U8, name="scale_table", align_bytes=64, offset=AT_SCALES)
         nc.gpsimd.memset(scale_table[:].bitcast(I32), 0)
         nc.vector.memset(t_table[0 : P - 1, :], 0.0)
 
         c_cols = keep.tile([P, BLOCKS], F32, name="c_cols")
 
         word_table = [keep.tile([P, T], U32, name="word_table%d" % z, align_bytes=64) for z in range(PASSES)]
-        w_raw = [keep.tile([P, PACK, N], F32, name="w_raw%d" % z, tag="w_raw%d" % z, align_bytes=64) for z in range(PASSES)]
+        w_raw = [shared.tile([P, PACK, N], F32, name="w_raw%d" % z, align_bytes=64, offset=AT_RAW[z]) for z in range(PASSES)]
 
         def load_words(z):
             nc.sync.dma_start(word_table[z][:].bitcast(I32), x_words[z].rearrange("p n t -> p (n t)").bitcast(I32))
@@ -71,7 +77,7 @@ def tile_picked_tokscale_relu_p_kernel(tc, x_words, x_scales, tscale, cscale, w1
         identity = keep.tile([P, P], F32, name="identity", align_bytes=64)
         make_identity(nc, identity[:])
 
-        t_row = keep.tile([P, S], F32, name="t_row", tag="slot_a", align_bytes=64)
+        t_row = shared.tile([P, S], F32, name="t_row", align_bytes=64, offset=AT_ROW)
         nc.vector.tensor_copy(t_row[:], t_table[:].indirect(offsets[:]))
         x_first = keep.tile([P, S], U32, name="x_first", align_bytes=64)
         nc.vector.tensor_copy(x_first[:], word_table[0][:].indirect(offsets[:]))
@@ -90,19 +96,22 @@ def tile_picked_tokscale_relu_p_kernel(tc, x_words, x_scales, tscale, cscale, w1
             )
 
         def quantize(z, b, grouped):
-            w_codes[z, b] = keep.tile([P, P], U32, name="w_codes%d_%d" % (z, b * P), align_bytes=64)
-            w_scale[z, b] = keep.tile([P, P], U8, name="w_scale%d_%d" % (z, b * P), align_bytes=64)
+            w_codes[z, b] = keep.tile([P, P], U32, name="w_codes%d_%d" % (z, b), align_bytes=64)
+            w_scale[z, b] = shared.tile(
+                [P, P], U8, name="w_scale%d_%d" % (z, b), align_bytes=64, offset=AT_SCALES + (BLOCKS * z + b) * P
+            )
             nc.vector.quantize_mx(w_codes[z, b][:].bitcast(FP8X4), w_scale[z, b][:], grouped.rearrange("p m t -> p (m t)"))
 
-        def multiply(z, b, h, words):
+        def multiply(z, b, first, width, words):
+            start, bank = [(piece[1], acc[piece]) for piece in PIECES if piece[0] == b and piece[1] <= first][-1]
             nc.tensor.matmul_mx(
-                acc[b, h][:],
+                bank[:, first - start : first - start + width],
                 lhsT=w_codes[z, b][:].bitcast(FP8X4),
                 lhsT_scale=w_scale[z, b][:],
-                rhs=words[:, h * HALF : (h + 1) * HALF].bitcast(FP8X4),
-                rhs_scale=x_scale[PACK * z :, h * HALF : (h + 1) * HALF],
+                rhs=words[:, first : first + width].bitcast(FP8X4),
+                rhs_scale=x_scale[PACK * z :, first : first + width],
                 start=(z == 0),
-                stop=(z == PASSES - 1),
+                stop=(z == PASSES - 1 and first - start + width == bank.shape[1]),
             )
 
         turned = psum.tile([P, S // P, P], F32, name="turned")
@@ -114,56 +123,49 @@ def tile_picked_tokscale_relu_p_kernel(tc, x_words, x_scales, tscale, cscale, w1
         for j in range(S // P):
             nc.tensor.transpose(spread[:, j, :], t_cols[:, j : j + 1].to_broadcast([P, P]), identity[:])
 
-        for b in range(BLOCKS):
-            for h in range(HALVES):
-                acc[b, h] = psum.tile([P, HALF], F32, name="acc%d%d" % (b, h))
+        for piece in PIECES:
+            acc[piece] = psum.tile([P, piece[2]], F32, name="acc%d_%d" % piece[0:2])
 
-        grouped_first = keep.tile([P, N, PACK], BF16, name="grouped0_0", tag="slot_a", align_bytes=64)
-        split = N - VECTOR_SHARE[0]
+        grouped_first = shared.tile([P, N, PACK], BF16, name="grouped_first", align_bytes=64, offset=AT_ROW - 1024)
         lay_out(nc.scalar.copy, grouped_first[:, 0:P, :], 0, 0)
+        split = N - VECTOR_SHARE[0]
         lay_out(nc.scalar.copy, grouped_first[:, P:split, :], 0, P)
         lay_out(nc.vector.tensor_copy, grouped_first[:, split:N, :], 0, split)
         quantize(0, 0, grouped_first[:, 0:P, :])
 
-        grouped_low = keep.tile([P, P, PACK], BF16, name="grouped1_0", tag="slot_b", align_bytes=64)
+        grouped_low = shared.tile([P, P, PACK], BF16, name="grouped_low", align_bytes=64, offset=AT_ROW + 1024)
         lay_out(nc.scalar.copy, grouped_low[:], 1, 0)
-        grouped_high = keep.tile([P, P, PACK], BF16, name="grouped1_128", tag="w_raw0", align_bytes=64)
+        grouped_high = shared.tile([P, P, PACK], BF16, name="grouped_high", align_bytes=64, offset=AT_SCALES + T // 2)
         split = P - VECTOR_SHARE[1]
         lay_out(nc.scalar.copy, grouped_high[:, 0:split, :], 1, P)
         lay_out(nc.vector.tensor_copy, grouped_high[:, split:P, :], 1, P + split)
         quantize(0, 1, grouped_first[:, P:N, :])
-
-        for h in range(HALVES):
-            for b in range(BLOCKS):
-                multiply(0, b, h, x_first)
-
+        for b, first, width in sorted(PIECES):
+            multiply(0, b, first, width, x_first)
         quantize(1, 0, grouped_low[:])
         quantize(1, 1, grouped_high[:])
 
-        t_picked = keep.tile([P, S], F32, name="t_picked", tag="slot_b", align_bytes=64)
+        t_picked = shared.tile([P, S], F32, name="t_picked", align_bytes=64, offset=AT_RAW[1] + 4 * S)
         nc.scalar.activation(t_picked[:], spread[:].rearrange("p j n -> p (j n)"), COPY)
 
-        x_second = keep.tile([P, S], U32, name="x_second", tag="w_raw1", align_bytes=64)
-        for h in range(HALVES):
+        x_second = shared.tile([P, S], U32, name="x_second", align_bytes=64, offset=AT_RAW[1])
+        for q in range(QUARTERS):
             nc.vector.tensor_copy(
-                x_second[:, h * HALF : (h + 1) * HALF],
-                word_table[1][:].indirect(offsets[:, h * HALF // ENTRIES : (h + 1) * HALF // ENTRIES]),
+                x_second[:, q * P : (q + 1) * P],
+                word_table[1][:].indirect(offsets[:, q * P // ENTRIES : (q + 1) * P // ENTRIES]),
             )
             for b in range(BLOCKS):
-                multiply(1, b, h, x_second)
+                multiply(1, b, q * P, P, x_second)
 
-        def finish(b, h, start, width):
-            column = h * HALF + start
-            scaled = keep.tile([P, width], F32, name="scaled%d_%d" % (b, column), align_bytes=64)
-            nc.vector.scalar_tensor_tensor(
-                scaled[:], acc[b, h][:, start : start + width], c_cols[:, b : b + 1], t_picked[:, column : column + width], MULT, MULT
-            )
-            result = keep.tile([P, width], F32, name="result%d_%d" % (b, column), align_bytes=64)
-            nc.scalar.activation(result[:], scaled[:], RELU)
-            nc.sync.dma_start(out[b * P : (b + 1) * P, column : column + width], result[:])
-
-        finish(0, 0, 0, HALF)
-        finish(1, 0, 0, HALF)
-        finish(0, 1, 0, HALF)
-        finish(1, 1, 0, HALF // 2)
-        finish(1, 1, HALF // 2, HALF // 2)
+        scaled = [keep.tile([P, S], F32, name="scaled%d" % b, align_bytes=64) for b in range(BLOCKS)]
+        for b, first, width in PIECES:
+            columns = slice(first, first + width)
+            nc.vector.tensor_tensor(scaled[b][:, columns], acc[b, first, width][:], t_picked[:, columns], MULT)
+            if (first + width) % HALF == 0:
+                columns = slice(first + width - HALF, first + width)
+                result = keep.tile([P, HALF], F32, name="result%d_%d" % (b, first), align_bytes=64)
+                if (b, first, width) != PIECES[-1]:
+                    nc.scalar.activation(result[:], scaled[b][:, columns], RELU, scale=c_cols[:, b : b + 1])
+                else:
+                    nc.vector.tensor_scalar(result[:], scaled[b][:, columns], c_cols[:, b : b + 1], 0.0, MULT, MAX)
+                nc.sync.dma_start(out[b * P : (b + 1) * P, columns], result[:])

@@ -158,14 +158,17 @@ def tile_picked_tokscale_relu_p_kernel(tc, x_words, x_scales, tscale, cscale, w1
                 multiply(1, b, q * P, P, x_second)
 
         scaled = [keep.tile([P, S], F32, name="scaled%d" % b, align_bytes=64) for b in range(BLOCKS)]
-        for b, first, width in PIECES:
-            columns = slice(first, first + width)
-            nc.vector.tensor_tensor(scaled[b][:, columns], acc[b, first, width][:], t_picked[:, columns], MULT)
-            if (first + width) % HALF == 0:
-                columns = slice(first + width - HALF, first + width)
-                result = keep.tile([P, HALF], F32, name="result%d_%d" % (b, first), align_bytes=64)
-                if (b, first, width) != PIECES[-1]:
-                    nc.scalar.activation(result[:], scaled[b][:, columns], RELU, scale=c_cols[:, b : b + 1])
+        result = [keep.tile([P, S], F32, name="result%d" % b, align_bytes=64) for b in range(BLOCKS)]
+        for b, start, width in PIECES:
+            quarters = [slice(first, first + P) for first in range(start, start + width, P)]
+            for columns in quarters:
+                bank = acc[b, start, width][:, columns.start - start : columns.stop - start]
+                nc.vector.tensor_tensor(scaled[b][:, columns], bank, t_picked[:, columns], MULT)
+            for columns in quarters:
+                if (b, start, width) != PIECES[-1]:
+                    nc.scalar.activation(result[b][:, columns], scaled[b][:, columns], RELU, scale=c_cols[:, b : b + 1])
                 else:
-                    nc.vector.tensor_scalar(result[:], scaled[b][:, columns], c_cols[:, b : b + 1], 0.0, MULT, MAX)
-                nc.sync.dma_start(out[b * P : (b + 1) * P, columns], result[:])
+                    nc.vector.tensor_scalar(result[b][:, columns], scaled[b][:, columns], c_cols[:, b : b + 1], 0.0, MULT, MAX)
+            if (start + width) % HALF == 0:
+                columns = slice(start + width - HALF, start + width)
+                nc.sync.dma_start(out[b * P : (b + 1) * P, columns], result[b][:, columns])

@@ -29,6 +29,7 @@ QUARTERS = S // P
 HALF = S // 2
 PIECES = [(0, 0, P), (0, P, P), (1, 0, HALF), (0, HALF, P), (0, HALF + P, P), (1, HALF, HALF)]
 VECTOR_SHARE = (64, 96)
+VECTOR_RELUS = 3
 AT_SCALES = 0
 AT_RAW = (1024, 6144)
 AT_ROW = 11264
@@ -159,16 +160,15 @@ def tile_picked_tokscale_relu_p_kernel(tc, x_words, x_scales, tscale, cscale, w1
 
         scaled = [keep.tile([P, S], F32, name="scaled%d" % b, align_bytes=64) for b in range(BLOCKS)]
         result = [keep.tile([P, S], F32, name="result%d" % b, align_bytes=64) for b in range(BLOCKS)]
-        for b, start, width in PIECES:
-            quarters = [slice(first, first + P) for first in range(start, start + width, P)]
-            for columns in quarters:
-                bank = acc[b, start, width][:, columns.start - start : columns.stop - start]
-                nc.vector.tensor_tensor(scaled[b][:, columns], bank, t_picked[:, columns], MULT)
-            for columns in quarters:
-                if (b, start, width) != PIECES[-1]:
-                    nc.scalar.activation(result[b][:, columns], scaled[b][:, columns], RELU, scale=c_cols[:, b : b + 1])
-                else:
-                    nc.vector.tensor_scalar(result[b][:, columns], scaled[b][:, columns], c_cols[:, b : b + 1], 0.0, MULT, MAX)
-            if (start + width) % HALF == 0:
-                columns = slice(start + width - HALF, start + width)
+        quarters = [(piece, slice(first, first + P)) for piece in PIECES for first in range(piece[1], piece[1] + piece[2], P)]
+        for (b, start, width), columns in quarters:
+            bank = acc[b, start, width][:, columns.start - start : columns.stop - start]
+            nc.vector.tensor_tensor(scaled[b][:, columns], bank, t_picked[:, columns], MULT)
+        for n, ((b, start, width), columns) in enumerate(quarters):
+            if n < len(quarters) - VECTOR_RELUS:
+                nc.scalar.activation(result[b][:, columns], scaled[b][:, columns], RELU, scale=c_cols[:, b : b + 1])
+            else:
+                nc.vector.tensor_scalar(result[b][:, columns], scaled[b][:, columns], c_cols[:, b : b + 1], 0.0, MULT, MAX)
+            if n < 2 or n % 2 == 1:
+                columns = columns if n < 2 else slice(columns.stop - HALF, columns.stop)
                 nc.sync.dma_start(out[b * P : (b + 1) * P, columns], result[b][:, columns])

@@ -46,7 +46,7 @@ def tile_picked_tokscale_relu_p_kernel(tc, x_words, x_scales, tscale, cscale, w1
         nc.sync.dma_start(offsets[:], offs)
 
         t_table = keep.tile([P, T], F32, name="t_table", align_bytes=64)
-        nc.sync.dma_start(t_table[P - 1 : P, :], tscale[0:1, :])
+        nc.scalar.dma_start(t_table[P - 1 : P, :], tscale[0:1, :])
 
         scale_table = shared.tile([P, T], U8, name="scale_table", align_bytes=64, offset=AT_SCALES)
         nc.gpsimd.memset(scale_table[:].bitcast(I32), 0)

@@ -49,7 +49,7 @@ def tile_picked_tokscale_relu_p_kernel(tc, x_words, x_scales, tscale, cscale, w1
         nc.scalar.dma_start(t_table[P - 1 : P, :], tscale[0:1, :])
 
         scale_table = shared.tile([P, T], U8, name="scale_table", align_bytes=64, offset=AT_SCALES)
-        nc.gpsimd.memset(scale_table[:].bitcast(I32), 0)
+        nc.vector.memset(scale_table[:].bitcast(I32), 0)
         nc.vector.memset(t_table[0 : P - 1, :], 0.0)
 
         c_cols = keep.tile([P, BLOCKS], F32, name="c_cols")

from contextlib import ExitStack

import concourse.mybir as mybir
from concourse.masks import make_identity

K, T, S, N = 1024, 1024, 512, 256
FLOPS = 2 * K * S * N

F32 = mybir.dt.float32
BF16 = mybir.dt.bfloat16
I32 = mybir.dt.int32
U32 = mybir.dt.uint32
U16 = mybir.dt.uint16
U8 = mybir.dt.uint8
FP8X4 = mybir.dt.float8_e4m3fn_x4
MULT = mybir.AluOpType.mult
MAX = mybir.AluOpType.max
COPY = mybir.ActivationFunctionType.Copy
RELU = mybir.ActivationFunctionType.Relu

P = 128
PACK = 4
QUADRANT = 32
ENTRIES = 16
K_PASS = P * PACK
PASSES = K // K_PASS
BLOCKS = N // P
QUARTERS = S // P
HALF = S // 2
PIECES = [(0, 0, P), (0, P, P), (1, 0, HALF), (0, HALF, P), (0, HALF + P, P), (1, HALF, HALF)]
VECTOR_SHARE = (64, 96)
VECTOR_RELUS = 3
AT_SCALES = 0
AT_RAW = (1024, 6144)
AT_ROW = 11264


def tile_picked_tokscale_relu_p_kernel(tc, x_words, x_scales, tscale, cscale, w1, offs, out):
    nc = tc.nc
    with ExitStack() as ctx:
        keep = ctx.enter_context(tc.tile_pool(name="keep", bufs=1))
        shared = ctx.enter_context(tc.tile_pool(name="shared", bufs=1))
        psum = ctx.enter_context(tc.psum_pool(name="psum", bufs=1))

        offsets = keep.tile([P, S // ENTRIES], U16, name="offsets")
        nc.sync.dma_start(offsets[:], offs)

        t_table = keep.tile([P, T], F32, name="t_table", align_bytes=64)
        nc.scalar.dma_start(t_table[P - 1 : P, :], tscale[0:1, :])

        scale_table = shared.tile([P, T], U8, name="scale_table", align_bytes=64, offset=AT_SCALES)
        nc.vector.memset(scale_table[:].bitcast(I32), 0)
        nc.vector.memset(t_table[0 : P - 1, :], 0.0)

        c_cols = keep.tile([P, BLOCKS], F32, name="c_cols")

        word_table = [keep.tile([P, T], U32, name="word_table%d" % z, align_bytes=64) for z in range(PASSES)]
        w_raw = [shared.tile([P, PACK, N], F32, name="w_raw%d" % z, align_bytes=64, offset=AT_RAW[z]) for z in range(PASSES)]

        def load_words(z):
            nc.sync.dma_start(word_table[z][:].bitcast(I32), x_words[z].rearrange("p n t -> p (n t)").bitcast(I32))

        def load_weights(z):
            nc.sync.dma_start(w_raw[z][:], w1[z * K_PASS : (z + 1) * K_PASS, :].rearrange("(p j) m -> p j m", j=PACK))

        load_words(0)
        for q in range(P // QUADRANT):
            nc.sync.dma_start(
                scale_table[QUADRANT * q : QUADRANT * q + PACK * PASSES, :].bitcast(I32),
                x_scales[:, PACK * q : PACK * (q + 1), :].bitcast(I32),
            )
        load_weights(0)
        load_weights(1)
        load_words(1)
        with nc.allow_non_contiguous_dma(reason="256 channel scales, one a partition"):
            nc.sync.dma_start(c_cols[:], cscale.rearrange("(b p) o -> p (b o)", p=P))

        identity = keep.tile([P, P], F32, name="identity", align_bytes=64)
        make_identity(nc, identity[:])

        t_row = shared.tile([P, S], F32, name="t_row", align_bytes=64, offset=AT_ROW)
        nc.vector.tensor_copy(t_row[:], t_table[:].indirect(offsets[:]))
        x_first = keep.tile([P, S], U32, name="x_first", align_bytes=64)
        nc.vector.tensor_copy(x_first[:], word_table[0][:].indirect(offsets[:]))
        x_scale = keep.tile([P, S], U8, name="x_scale", align_bytes=64)
        nc.vector.tensor_copy(x_scale[:], scale_table[:].indirect(offsets[:]))

        w_codes = {}
        w_scale = {}
        acc = {}

        def lay_out(copy, grouped, z, channel):
            width = grouped.shape[1]
            copy(
                grouped.rearrange("p (c i) t -> p c t i", i=PACK),
                w_raw[z][:, :, channel : channel + width].rearrange("p t (c i) -> p c t i", i=PACK),
            )

        def quantize(z, b, grouped):
            w_codes[z, b] = keep.tile([P, P], U32, name="w_codes%d_%d" % (z, b), align_bytes=64)
            w_scale[z, b] = shared.tile(
                [P, P], U8, name="w_scale%d_%d" % (z, b), align_bytes=64, offset=AT_SCALES + (BLOCKS * z + b) * P
            )
            nc.vector.quantize_mx(w_codes[z, b][:].bitcast(FP8X4), w_scale[z, b][:], grouped.rearrange("p m t -> p (m t)"))

        def multiply(z, b, first, width, words):
            start, bank = [(piece[1], acc[piece]) for piece in PIECES if piece[0] == b and piece[1] <= first][-1]
            nc.tensor.matmul_mx(
                bank[:, first - start : first - start + width],
                lhsT=w_codes[z, b][:].bitcast(FP8X4),
                lhsT_scale=w_scale[z, b][:],
                rhs=words[:, first : first + width].bitcast(FP8X4),
                rhs_scale=x_scale[PACK * z :, first : first + width],
                start=(z == 0),
                stop=(z == PASSES - 1 and first - start + width == bank.shape[1]),
            )

        turned = psum.tile([P, S // P, P], F32, name="turned")
        for j in range(S // P):
            nc.tensor.transpose(turned[:, j, :], t_row[:, j * P : (j + 1) * P], identity[:])
        t_cols = keep.tile([P, S // P], F32, name="t_cols", align_bytes=64)
        nc.scalar.activation(t_cols[:], turned[:, :, P - 1], COPY)
        spread = psum.tile([P, S // P, P], F32, name="spread")
        for j in range(S // P):
            nc.tensor.transpose(spread[:, j, :], t_cols[:, j : j + 1].to_broadcast([P, P]), identity[:])

        for piece in PIECES:
            acc[piece] = psum.tile([P, piece[2]], F32, name="acc%d_%d" % piece[0:2])

        grouped_first = shared.tile([P, N, PACK], BF16, name="grouped_first", align_bytes=64, offset=AT_ROW - 1024)
        lay_out(nc.scalar.copy, grouped_first[:, 0:P, :], 0, 0)
        split = N - VECTOR_SHARE[0]
        lay_out(nc.scalar.copy, grouped_first[:, P:split, :], 0, P)
        lay_out(nc.vector.tensor_copy, grouped_first[:, split:N, :], 0, split)
        quantize(0, 0, grouped_first[:, 0:P, :])

        grouped_low = shared.tile([P, P, PACK], BF16, name="grouped_low", align_bytes=64, offset=AT_ROW + 1024)
        lay_out(nc.scalar.copy, grouped_low[:], 1, 0)
        grouped_high = shared.tile([P, P, PACK], BF16, name="grouped_high", align_bytes=64, offset=AT_SCALES + T // 2)
        split = P - VECTOR_SHARE[1]
        lay_out(nc.scalar.copy, grouped_high[:, 0:split, :], 1, P)
        lay_out(nc.vector.tensor_copy, grouped_high[:, split:P, :], 1, P + split)
        quantize(0, 1, grouped_first[:, P:N, :])
        for b, first, width in sorted(PIECES):
            multiply(0, b, first, width, x_first)
        quantize(1, 0, grouped_low[:])
        quantize(1, 1, grouped_high[:])

        t_picked = shared.tile([P, S], F32, name="t_picked", align_bytes=64, offset=AT_RAW[1] + 4 * S)
        nc.scalar.activation(t_picked[:], spread[:].rearrange("p j n -> p (j n)"), COPY)

        x_second = shared.tile([P, S], U32, name="x_second", align_bytes=64, offset=AT_RAW[1])
        for q in range(QUARTERS):
            nc.vector.tensor_copy(
                x_second[:, q * P : (q + 1) * P],
                word_table[1][:].indirect(offsets[:, q * P // ENTRIES : (q + 1) * P // ENTRIES]),
            )
            for b in range(BLOCKS):
                multiply(1, b, q * P, P, x_second)

        scaled = [keep.tile([P, S], F32, name="scaled%d" % b, align_bytes=64) for b in range(BLOCKS)]
        result = [keep.tile([P, S], F32, name="result%d" % b, align_bytes=64) for b in range(BLOCKS)]
        quarters = [(piece, slice(first, first + P)) for piece in PIECES for first in range(piece[1], piece[1] + piece[2], P)]
        for (b, start, width), columns in quarters:
            bank = acc[b, start, width][:, columns.start - start : columns.stop - start]
            nc.vector.tensor_tensor(scaled[b][:, columns], bank, t_picked[:, columns], MULT)
        for n, ((b, start, width), columns) in enumerate(quarters):
            if n < len(quarters) - VECTOR_RELUS:
                nc.scalar.activation(result[b][:, columns], scaled[b][:, columns], RELU, scale=c_cols[:, b : b + 1])
            else:
                nc.vector.tensor_scalar(result[b][:, columns], scaled[b][:, columns], c_cols[:, b : b + 1], 0.0, MULT, MAX)
            if n < 2 or n % 2 == 1:
                columns = columns if n < 2 else slice(columns.stop - HALF, columns.stop)
                nc.sync.dma_start(out[b * P : (b + 1) * P, columns], result[b][:, columns])
